import numpy as np
import ml_dtypes


def mxq(x, axis, fmt="e4m3"):
    dtype, down = {"e4m3": (ml_dtypes.float8_e4m3fn, 7), "e5m2": (ml_dtypes.float8_e5m2, 14)}[fmt]
    v = np.moveaxis(np.asarray(x, np.float32).astype(ml_dtypes.bfloat16).astype(np.float64), axis, -1)
    blocks = v.reshape(v.shape[:-1] + (-1, 32))
    amax = np.abs(blocks).max(-1, keepdims=True)
    byte = np.maximum(np.where(amax > 0, np.frexp(amax)[1] - 1 + 127, 0) - down, 1)
    scale = np.exp2(byte - 127.0)
    codes = (blocks / scale).astype(np.float32).astype(dtype).astype(np.float64)
    return np.moveaxis((codes * scale).reshape(v.shape), -1, axis)


WIDE = False


def mx_kscale(k):
    if not WIDE:
        return np.ones(k)
    levels = np.array([10, -10, 5, -5, 0])
    if k % 512:
        return np.exp2(np.random.permutation(np.resize(levels, k // 32))).repeat(32)
    a = np.empty((k // 512, 16))
    for p in range(k // 512):
        a[p, :8] = np.random.permutation(np.resize(levels, 8))
        for g in range(8):
            far = levels[np.abs(levels - a[p, g]) >= 10]
            a[p, g + 8] = far[np.random.randint(len(far))]
    return np.exp2(a.ravel()).repeat(32)


def f64(x):
    return np.asarray(x).astype(np.float64)


def striped(idx):
    return np.tile(idx.reshape(-1, 16).T, (8, 1)).astype(np.uint16)


def unstriped(offs):
    return offs[:16].T.reshape(-1).astype(np.int64)


def pack_weight(w):
    k, n = w.shape
    w = f64(np.asarray(w, np.float32).astype(ml_dtypes.bfloat16)).reshape(k // 32, 32, n)
    amax = np.abs(w).max(1)
    byte = np.clip(np.where(amax > 0, np.frexp(amax)[1] - 1 + 127 - 7, 1), 1, 254)
    scaled = (w * np.exp2(127.0 - byte)[:, None, :]).reshape(k, n).astype(np.float32)
    words = np.ascontiguousarray(scaled.reshape(k // 512, 128, 4, n).transpose(0, 1, 3, 2)).astype(ml_dtypes.float8_e4m3fn).view(np.uint8)
    return words, np.ascontiguousarray(byte.astype(np.uint8).reshape(k // 512, 16, n))


def unpack_weight(words, scales):
    g, p, n, _ = words.shape
    vals = np.ascontiguousarray(words).view(ml_dtypes.float8_e4m3fn).astype(np.float64) * np.repeat(np.exp2(scales.astype(np.float64) - 127.0), 8, axis=1)[..., None]
    return vals.transpose(0, 1, 3, 2).reshape(g * 512, n)


def gelu(v):
    return 0.5 * v * (1.0 + np.tanh(np.sqrt(2.0 / np.pi) * (v + 0.044715 * v**3)))


K, T, S, V, H, N = 512, 4096, 1536, 384, 512, 128


def setup_inputs():
    n = np.random.standard_normal
    s = mx_kscale(K)[:, None]
    u = mx_kscale(H)
    packed_xT = pack_weight(n((K, T)) * s)
    return {
        "x_words": packed_xT[0],
        "x_scales": packed_xT[1],
        "w1": (n((K, H)) / np.sqrt(K) / s * u).astype(np.float32),
        "w2": (n((H, N)) / np.sqrt(2 * H) / u[:, None]).astype(np.float32),
        "w3": (n((H, N)) / np.sqrt(2 * H) / u[:, None]).astype(np.float32),
        "offs": striped(np.random.permutation(T)[:S]),
    }


def reference(x_words, x_scales, w1, w2, w3, offs):
    xq = unpack_weight(x_words, x_scales)[:, unstriped(offs)]
    h = gelu(mxq(f64(w1), 0, "e4m3").T @ xq)
    mean = (h[:, :V] + h[:, V:2 * V] + h[:, 2 * V:3 * V] + h[:, 3 * V:4 * V]) / 4
    dev = np.sqrt(((h[:, :V] - mean) ** 2 + (h[:, V:2 * V] - mean) ** 2 + (h[:, 2 * V:3 * V] - mean) ** 2 + (h[:, 3 * V:4 * V] - mean) ** 2) / 4)
    return mxq(f64(w2), 0, "e4m3").T @ mxq(mean, 0, "e4m3") + mxq(f64(w3), 0, "e4m3").T @ mxq(dev, 0, "e4m3")

@@ -1,0 +1,228 @@
+from contextlib import ExitStack
+
+import concourse.mybir as mybir
+from concourse.masks import make_identity
+
+K, T, S, V, H, N = 512, 4096, 1536, 384, 512, 128
+D = S // V
+FLOPS = 2 * K * H * S + 2 * 2 * H * N * V
+
+F32 = mybir.dt.float32
+BF16 = mybir.dt.bfloat16
+I32 = mybir.dt.int32
+U32 = mybir.dt.uint32
+U16 = mybir.dt.uint16
+U8 = mybir.dt.uint8
+FP8X4 = mybir.dt.float8_e4m3fn_x4
+ACT = mybir.ActivationFunctionType
+ALU = mybir.AluOpType
+
+P = 128
+PACK = 4
+GATHER = 512
+TILES = V // P
+SQRT_FLOOR = 2.0**-116
+
+
+def tile_picked_statpool_gelu_p_kernel(tc, x_words, x_scales, w1, w2, w3, offs, out):
+    nc = tc.nc
+    with ExitStack() as ctx:
+        keep = ctx.enter_context(tc.tile_pool(name="keep", bufs=1))
+        psum = ctx.enter_context(tc.psum_pool(name="psum", bufs=1))
+
+        offsets = keep.tile([P, S // 16], U16, name="offsets")
+        word_table = keep.tile([P, T], U32, name="word_table", align_bytes=64)
+        scale_table = keep.tile([P, T], U8, name="scale_table", align_bytes=64)
+        w1_raw = keep.tile([P, PACK, H], F32, name="w1_raw", align_bytes=64)
+        w23_raw = [keep.tile([P, PACK, N], F32, name=f"w{2 + s}_raw", align_bytes=64) for s in range(2)]
+
+        nc.vector.memset(scale_table[:].bitcast(I32), 0)
+        nc.sync.dma_start(offsets[:], offs)
+        nc.sync.dma_start(out=w1_raw[:], in_=w1.rearrange("(p j) c -> p j c", j=PACK))
+        for q in range(4):
+            nc.sync.dma_start(
+                out=scale_table[32 * q : 32 * q + 4, :].bitcast(I32),
+                in_=x_scales[0, 4 * q : 4 * q + 4, :].bitcast(I32),
+            )
+        nc.sync.dma_start(
+            out=word_table[:].bitcast(I32),
+            in_=x_words[0].rearrange("p n t -> p (n t)").bitcast(I32),
+        )
+        for s, w in enumerate((w2, w3)):
+            nc.sync.dma_start(out=w23_raw[s][:], in_=w.rearrange("(p t) n -> p t n", t=PACK))
+
+        identity = keep.tile([P, P], F32, name="identity", align_bytes=64)
+        make_identity(nc, identity[:])
+        warm = keep.tile([P, 1], F32, name="warm")
+        nc.scalar.activation(out=warm[:], in_=identity[:, 0:1], func=ACT.Gelu_apprx_tanh)
+
+        def list_slice(g):
+            return offsets[:, g * GATHER // 16 : (g + 1) * GATHER // 16]
+
+        x_codes = [keep.tile([P, GATHER], U32, name=f"x_codes{g}", align_bytes=64) for g in range(S // GATHER)]
+        x_planes = [keep.tile([P, GATHER], U8, name=f"x_planes{g}", align_bytes=64) for g in range(S // GATHER)]
+        for g in range(S // GATHER):
+            nc.vector.tensor_copy(out=x_planes[g][:], in_=scale_table[:].indirect(list_slice(g)))
+
+        w1_bf = keep.tile([P, H * PACK], BF16, name="w1_bf", align_bytes=64)
+        nc.scalar.copy(
+            out=w1_bf[:].rearrange("p (t m j) -> p m j t", t=PACK, j=PACK),
+            in_=w1_raw[:].rearrange("p j (m t) -> p m j t", t=PACK),
+        )
+        w1_codes = keep.tile([P, H], U32, name="w1_codes", align_bytes=64)
+        w1_plane = keep.tile([P, H], U8, name="w1_plane", align_bytes=64)
+        nc.vector.quantize_mx(out=w1_codes[:].bitcast(FP8X4), scales=w1_plane[:], in_=w1_bf[:])
+
+        for g in range(S // GATHER):
+            nc.vector.tensor_copy(out=x_codes[g][:], in_=word_table[:].indirect(list_slice(g)))
+
+        w23_bf = keep.tile([P, 2, N * PACK], BF16, name="w23_bf", align_bytes=64)
+        for s in range(2):
+            nc.gpsimd.tensor_scalar(
+                out=w23_bf[:, s, :].rearrange("p (n t) -> p n t", t=PACK),
+                in0=w23_raw[s][:].rearrange("p t n -> p n t"),
+                scalar1=1.0,
+                scalar2=0.0,
+                op0=ALU.mult,
+                op1=ALU.add,
+            )
+        w23_codes = keep.tile([P, 2 * N], U32, name="w23_codes", align_bytes=64)
+        w23_plane = keep.tile([P, 2 * N], U8, name="w23_plane", align_bytes=64)
+
+        def wide(name):
+            return keep.tile([P, H], F32, name=name, align_bytes=64)
+
+        h = {}
+        val = {}
+        banks = {}
+
+        def hidden(d, vt):
+            g, col = divmod(d * V + vt * P, GATHER)
+            pre = psum.tile([P, H], F32, name=f"pre{d}_{vt}", tag="pre", bufs=3)
+            nc.tensor.matmul_mx(
+                out=pre[:],
+                lhsT=x_codes[g][:, col : col + P].bitcast(FP8X4),
+                lhsT_scale=x_planes[g][:, col : col + P],
+                rhs=w1_codes[:].bitcast(FP8X4),
+                rhs_scale=w1_plane[:],
+                start=True,
+                stop=True,
+            )
+            h[d, vt] = wide(f"h{d}_{vt}")
+            nc.scalar.activation(out=h[d, vt][:], in_=pre[:], func=ACT.Gelu_apprx_tanh)
+
+        def turn_and_add(bank, values, first, last):
+            for t in range(PACK):
+                nc.tensor.matmul(
+                    out=bank[:, t, :],
+                    lhsT=values[:, t * P : (t + 1) * P],
+                    rhs=identity[:],
+                    is_transpose=True,
+                    start=first and t == 0,
+                    stop=last and t == PACK - 1,
+                )
+
+        def combine(name, vt, x, y, op):
+            val[name, vt] = wide(f"{name}{vt}")
+            nc.vector.tensor_tensor(out=val[name, vt][:], in0=x[:], in1=y[:], op=op)
+
+        def first_pair(vt):
+            combine("b", vt, h[0, vt], h[1, vt], ALU.subtract)
+            combine("a", vt, h[0, vt], h[1, vt], ALU.add)
+
+        def first_square(vt):
+            val["bb", vt] = wide(f"bb{vt}")
+            nc.scalar.activation(out=val["bb", vt][:], in_=val["b", vt][:], func=ACT.Square)
+            banks["q", vt] = psum.tile([P, PACK, P], F32, name=f"squares{vt}", tag="squares", bufs=3)
+            turn_and_add(banks["q", vt], val["bb", vt], True, False)
+
+        def second_pair(vt):
+            combine("c", vt, h[2, vt], h[3, vt], ALU.add)
+            combine("e", vt, h[2, vt], h[3, vt], ALU.subtract)
+            banks["s", vt] = psum.tile([P, PACK, P], F32, name=f"sums{vt}", tag="sums", bufs=2)
+            turn_and_add(banks["s", vt], val["a", vt], True, False)
+            turn_and_add(banks["s", vt], val["c", vt], False, True)
+            combine("f", vt, val["a", vt], val["c", vt], ALU.subtract)
+            combine("ee", vt, val["e", vt], val["e", vt], ALU.mult)
+            turn_and_add(banks["q", vt], val["ee", vt], False, False)
+            val["ff", vt] = wide(f"ff{vt}")
+            nc.vector.scalar_tensor_tensor(
+                out=val["ff", vt][:], in0=val["f", vt][:], scalar=0.5, in1=val["f", vt][:], op0=ALU.mult, op1=ALU.mult
+            )
+            turn_and_add(banks["q", vt], val["ff", vt], False, True)
+
+        stat_bf = [keep.tile([P, 2, P * PACK], BF16, name=f"stat_bf{vt}", align_bytes=64) for vt in range(TILES)]
+        stat_codes = [keep.tile([P, 2 * P], U32, name=f"stat_codes{vt}", align_bytes=64) for vt in range(TILES)]
+        stat_plane = [keep.tile([P, 2 * P], U8, name=f"stat_plane{vt}", align_bytes=64) for vt in range(TILES)]
+
+        def quantize_stat(s, vt):
+            nc.vector.quantize_mx(
+                out=stat_codes[vt][:, s * P : (s + 1) * P].bitcast(FP8X4),
+                scales=stat_plane[vt][:, s * P : (s + 1) * P],
+                in_=stat_bf[vt][:, s, :],
+            )
+
+        def mean(vt):
+            nc.scalar.activation(
+                out=stat_bf[vt][:, 0, :].rearrange("p (v t) -> p v t", t=PACK),
+                in_=banks["s", vt][:].rearrange("p t v -> p v t"),
+                func=ACT.Copy,
+                scale=1.0 / D,
+            )
+            quantize_stat(0, vt)
+
+        def deviation(vt):
+            nc.scalar.activation(
+                out=stat_bf[vt][:, 1, :].rearrange("p (v t) -> p v t", t=PACK),
+                in_=banks["q", vt][:].rearrange("p t v -> p v t"),
+                func=ACT.Sqrt,
+                scale=1.0 / (2 * D),
+                bias=SQRT_FLOOR,
+            )
+            quantize_stat(1, vt)
+
+        def project(vt):
+            acc = psum.tile([P, H], F32, name=f"acc{vt}", tag="pre", bufs=3)
+            for s in range(2):
+                nc.tensor.matmul_mx(
+                    out=acc[:, :P],
+                    lhsT=w23_codes[:, s * N : (s + 1) * N].bitcast(FP8X4),
+                    lhsT_scale=w23_plane[:, s * N : (s + 1) * N],
+                    rhs=stat_codes[vt][:, s * P : (s + 1) * P].bitcast(FP8X4),
+                    rhs_scale=stat_plane[vt][:, s * P : (s + 1) * P],
+                    start=s == 0,
+                    stop=s == 1,
+                )
+            result = keep.tile([P, P], F32, name=f"result{vt}")
+            nc.vector.tensor_copy(out=result[:], in_=acc[:, :P])
+            nc.sync.dma_start(out=out[:, vt * P : (vt + 1) * P], in_=result[:])
+
+        for vt in range(2):
+            hidden(0, vt)
+            hidden(1, vt)
+            first_pair(vt)
+        hidden(2, 0)
+        hidden(3, 0)
+        first_square(0)
+        second_pair(0)
+        hidden(2, 1)
+        hidden(3, 1)
+        first_square(1)
+        second_pair(1)
+        nc.vector.quantize_mx(
+            out=w23_codes[:].bitcast(FP8X4), scales=w23_plane[:], in_=w23_bf[:].rearrange("p s c -> p (s c)")
+        )
+        for d in range(D):
+            hidden(d, 2)
+        mean(0)
+        first_pair(2)
+        first_square(2)
+        mean(1)
+        second_pair(2)
+        deviation(0)
+        project(0)
+        deviation(1)
+        project(1)
+        mean(2)
+        deviation(2)
+        project(2)

@@ -33,17 +33,19 @@ def tile_picked_statpool_gelu_p_kernel(tc, x_words, x_scales, w1, w2, w3, offs, 
         offsets = keep.tile([P, S // 16], U16, name="offsets")
         word_table = keep.tile([P, T], U32, name="word_table", align_bytes=64)
         scale_table = keep.tile([P, T], U8, name="scale_table", align_bytes=64)
-        w1_raw = keep.tile([P, PACK, H], F32, name="w1_raw", align_bytes=64)
+        w1_raw = [keep.tile([P, PACK, H // 2], F32, name=f"w1_raw{u}", align_bytes=64) for u in range(2)]
         w23_raw = [keep.tile([P, PACK, N], F32, name=f"w{2 + s}_raw", align_bytes=64) for s in range(2)]
 
         nc.vector.memset(scale_table[:].bitcast(I32), 0)
         nc.sync.dma_start(offsets[:], offs)
-        nc.sync.dma_start(out=w1_raw[:], in_=w1.rearrange("(p j) c -> p j c", j=PACK))
+        w1_rows = w1.rearrange("(p j) c -> p j c", j=PACK)
+        nc.sync.dma_start(out=w1_raw[0][:], in_=w1_rows[:, :, : H // 2])
         for q in range(4):
             nc.sync.dma_start(
                 out=scale_table[32 * q : 32 * q + 4, :].bitcast(I32),
                 in_=x_scales[0, 4 * q : 4 * q + 4, :].bitcast(I32),
             )
+        nc.sync.dma_start(out=w1_raw[1][:], in_=w1_rows[:, :, H // 2 :])
         nc.sync.dma_start(
             out=word_table[:].bitcast(I32),
             in_=x_words[0].rearrange("p n t -> p (n t)").bitcast(I32),
@@ -59,22 +61,26 @@ def tile_picked_statpool_gelu_p_kernel(tc, x_words, x_scales, w1, w2, w3, offs, 
         def list_slice(g):
             return offsets[:, g * GATHER // 16 : (g + 1) * GATHER // 16]
 
-        x_codes = [keep.tile([P, GATHER], U32, name=f"x_codes{g}", align_bytes=64) for g in range(S // GATHER)]
         x_planes = [keep.tile([P, GATHER], U8, name=f"x_planes{g}", align_bytes=64) for g in range(S // GATHER)]
         for g in range(S // GATHER):
             nc.vector.tensor_copy(out=x_planes[g][:], in_=scale_table[:].indirect(list_slice(g)))
 
-        w1_bf = keep.tile([P, H * PACK], BF16, name="w1_bf", align_bytes=64)
-        nc.scalar.copy(
-            out=w1_bf[:].rearrange("p (t m j) -> p m j t", t=PACK, j=PACK),
-            in_=w1_raw[:].rearrange("p j (m t) -> p m j t", t=PACK),
-        )
+        w1_bf = keep.tile([P, H * PACK], BF16, name="w1_bf", tag="w1_then_x", align_bytes=64)
+        w1_dealt = w1_bf[:].rearrange("p (t m j) -> p m j t", t=PACK, j=PACK)
+        for u in range(2):
+            nc.scalar.copy(
+                out=w1_dealt[:, u * P // 2 : (u + 1) * P // 2, :, :],
+                in_=w1_raw[u][:].rearrange("p j (m t) -> p m j t", t=PACK),
+            )
         w1_codes = keep.tile([P, H], U32, name="w1_codes", align_bytes=64)
         w1_plane = keep.tile([P, H], U8, name="w1_plane", align_bytes=64)
         nc.vector.quantize_mx(out=w1_codes[:].bitcast(FP8X4), scales=w1_plane[:], in_=w1_bf[:])
 
+        x_codes = keep.tile([P, S], U32, name="x_codes", tag="w1_then_x", align_bytes=64)
         for g in range(S // GATHER):
-            nc.vector.tensor_copy(out=x_codes[g][:], in_=word_table[:].indirect(list_slice(g)))
+            nc.vector.tensor_copy(
+                out=x_codes[:, g * GATHER : (g + 1) * GATHER], in_=word_table[:].indirect(list_slice(g))
+            )
 
         w23_bf = keep.tile([P, 2, N * PACK], BF16, name="w23_bf", align_bytes=64)
         for s in range(2):
@@ -97,11 +103,12 @@ def tile_picked_statpool_gelu_p_kernel(tc, x_words, x_scales, w1, w2, w3, offs, 
         banks = {}
 
         def hidden(d, vt):
-            g, col = divmod(d * V + vt * P, GATHER)
+            entry = d * V + vt * P
+            g, col = divmod(entry, GATHER)
             pre = psum.tile([P, H], F32, name=f"pre{d}_{vt}", tag="pre", bufs=3)
             nc.tensor.matmul_mx(
                 out=pre[:],
-                lhsT=x_codes[g][:, col : col + P].bitcast(FP8X4),
+                lhsT=x_codes[:, entry : entry + P].bitcast(FP8X4),
                 lhsT_scale=x_planes[g][:, col : col + P],
                 rhs=w1_codes[:].bitcast(FP8X4),
                 rhs_scale=w1_plane[:],
@@ -130,28 +137,32 @@ def tile_picked_statpool_gelu_p_kernel(tc, x_words, x_scales, w1, w2, w3, offs, 
             combine("b", vt, h[0, vt], h[1, vt], ALU.subtract)
             combine("a", vt, h[0, vt], h[1, vt], ALU.add)
 
-        def first_square(vt):
-            val["bb", vt] = wide(f"bb{vt}")
-            nc.scalar.activation(out=val["bb", vt][:], in_=val["b", vt][:], func=ACT.Square)
-            banks["q", vt] = psum.tile([P, PACK, P], F32, name=f"squares{vt}", tag="squares", bufs=3)
-            turn_and_add(banks["q", vt], val["bb", vt], True, False)
+        def add_square(name, vt, first, last):
+            if first:
+                banks["q", vt] = psum.tile([P, PACK, P], F32, name=f"squares{vt}", tag="squares", bufs=3)
+            turn_and_add(banks["q", vt], val[name, vt], first, last)
+
+        def scalar_square(name, vt):
+            val[2 * name, vt] = wide(f"{2 * name}{vt}")
+            nc.scalar.activation(out=val[2 * name, vt][:], in_=val[name, vt][:], func=ACT.Square)
 
         def second_pair(vt):
             combine("c", vt, h[2, vt], h[3, vt], ALU.add)
             combine("e", vt, h[2, vt], h[3, vt], ALU.subtract)
             banks["s", vt] = psum.tile([P, PACK, P], F32, name=f"sums{vt}", tag="sums", bufs=2)
-            turn_and_add(banks["s", vt], val["a", vt], True, False)
-            turn_and_add(banks["s", vt], val["c", vt], False, True)
+            turn_and_add(banks["s", vt], val["c", vt], True, False)
+            turn_and_add(banks["s", vt], val["a", vt], False, True)
             combine("f", vt, val["a", vt], val["c", vt], ALU.subtract)
-            combine("ee", vt, val["e", vt], val["e", vt], ALU.mult)
-            turn_and_add(banks["q", vt], val["ee", vt], False, False)
+
+        def half_square(vt):
             val["ff", vt] = wide(f"ff{vt}")
             nc.vector.scalar_tensor_tensor(
                 out=val["ff", vt][:], in0=val["f", vt][:], scalar=0.5, in1=val["f", vt][:], op0=ALU.mult, op1=ALU.mult
             )
-            turn_and_add(banks["q", vt], val["ff", vt], False, True)
 
-        stat_bf = [keep.tile([P, 2, P * PACK], BF16, name=f"stat_bf{vt}", align_bytes=64) for vt in range(TILES)]
+        mean_bf = keep.tile([P, TILES * H], BF16, name="mean_bf", align_bytes=64)
+        dev_bf = keep.tile([P, TILES * H], BF16, name="dev_bf", tag="w1_then_x", align_bytes=64)
+        stat_bf = (mean_bf, dev_bf)
         stat_codes = [keep.tile([P, 2 * P], U32, name=f"stat_codes{vt}", align_bytes=64) for vt in range(TILES)]
         stat_plane = [keep.tile([P, 2 * P], U8, name=f"stat_plane{vt}", align_bytes=64) for vt in range(TILES)]
 
@@ -159,27 +170,34 @@ def tile_picked_statpool_gelu_p_kernel(tc, x_words, x_scales, w1, w2, w3, offs, 
             nc.vector.quantize_mx(
                 out=stat_codes[vt][:, s * P : (s + 1) * P].bitcast(FP8X4),
                 scales=stat_plane[vt][:, s * P : (s + 1) * P],
-                in_=stat_bf[vt][:, s, :],
+                in_=stat_bf[s][:, vt * H : (vt + 1) * H],
             )
 
         def mean(vt):
             nc.scalar.activation(
-                out=stat_bf[vt][:, 0, :].rearrange("p (v t) -> p v t", t=PACK),
+                out=mean_bf[:, vt * H : (vt + 1) * H].rearrange("p (v t) -> p v t", t=PACK),
                 in_=banks["s", vt][:].rearrange("p t v -> p v t"),
                 func=ACT.Copy,
                 scale=1.0 / D,
             )
-            quantize_stat(0, vt)
+
+        def mean_on_vector(vt):
+            nc.vector.tensor_scalar(
+                out=mean_bf[:, vt * H : (vt + 1) * H].rearrange("p (v t) -> p v t", t=PACK),
+                in0=banks["s", vt][:].rearrange("p t v -> p v t"),
+                scalar1=1.0 / D,
+                scalar2=None,
+                op0=ALU.mult,
+            )
 
         def deviation(vt):
             nc.scalar.activation(
-                out=stat_bf[vt][:, 1, :].rearrange("p (v t) -> p v t", t=PACK),
+                out=dev_bf[:, vt * H : (vt + 1) * H].rearrange("p (v t) -> p v t", t=PACK),
                 in_=banks["q", vt][:].rearrange("p t v -> p v t"),
                 func=ACT.Sqrt,
                 scale=1.0 / (2 * D),
                 bias=SQRT_FLOOR,
             )
-            quantize_stat(1, vt)
 
         def project(vt):
             acc = psum.tile([P, H], F32, name=f"acc{vt}", tag="pre", bufs=3)
@@ -201,28 +219,48 @@ def tile_picked_statpool_gelu_p_kernel(tc, x_words, x_scales, w1, w2, w3, offs, 
             hidden(0, vt)
             hidden(1, vt)
             first_pair(vt)
-        hidden(2, 0)
-        hidden(3, 0)
-        first_square(0)
+        for vt in range(2):
+            hidden(2, vt)
+            hidden(3, vt)
         second_pair(0)
-        hidden(2, 1)
-        hidden(3, 1)
-        first_square(1)
+        combine("ee", 0, val["e", 0], val["e", 0], ALU.mult)
+        half_square(0)
+        for vt in range(2):
+            scalar_square("b", vt)
+            add_square("bb", vt, True, False)
+        add_square("ee", 0, False, False)
+        add_square("ff", 0, False, True)
+        hidden(0, 2)
+        hidden(1, 2)
         second_pair(1)
+        first_pair(2)
+        half_square(1)
+        add_square("ff", 1, False, False)
+        mean(0)
+        hidden(2, 2)
+        hidden(3, 2)
+        deviation(0)
+        scalar_square("e", 1)
+        add_square("ee", 1, False, True)
+        second_pair(2)
+        scalar_square("b", 2)
+        add_square("bb", 2, True, False)
+        mean(1)
         nc.vector.quantize_mx(
             out=w23_codes[:].bitcast(FP8X4), scales=w23_plane[:], in_=w23_bf[:].rearrange("p s c -> p (s c)")
         )
-        for d in range(D):
-            hidden(d, 2)
-        mean(0)
-        first_pair(2)
-        first_square(2)
-        mean(1)
-        second_pair(2)
-        deviation(0)
-        project(0)
+        half_square(2)
+        scalar_square("e", 2)
+        add_square("ff", 2, False, False)
+        add_square("ee", 2, False, True)
         deviation(1)
-        project(1)
-        mean(2)
         deviation(2)
+        for vt in range(2):
+            quantize_stat(0, vt)
+        mean_on_vector(2)
+        for vt in range(2):
+            quantize_stat(1, vt)
+            project(vt)
+        quantize_stat(0, 2)
+        quantize_stat(1, 2)
         project(2)

@@ -33,25 +33,22 @@ def tile_picked_statpool_gelu_p_kernel(tc, x_words, x_scales, w1, w2, w3, offs, 
         offsets = keep.tile([P, S // 16], U16, name="offsets")
         word_table = keep.tile([P, T], U32, name="word_table", align_bytes=64)
         scale_table = keep.tile([P, T], U8, name="scale_table", align_bytes=64)
-        w1_raw = [keep.tile([P, PACK, H // 2], F32, name=f"w1_raw{u}", align_bytes=64) for u in range(2)]
-        w23_raw = [keep.tile([P, PACK, N], F32, name=f"w{2 + s}_raw", align_bytes=64) for s in range(2)]
+        w1_raw = [
+            keep.tile([P, PACK, H // 2], F32, name=f"w1_raw{u}", tag=f"raw{u}", align_bytes=64) for u in range(2)
+        ]
+        x_plane = keep.tile([P, S], U8, name="x_plane", align_bytes=64)
 
         nc.vector.memset(scale_table[:].bitcast(I32), 0)
+        nc.gpsimd.memset(x_plane[:].bitcast(I32), 0)
         nc.sync.dma_start(offsets[:], offs)
         w1_rows = w1.rearrange("(p j) c -> p j c", j=PACK)
         nc.sync.dma_start(out=w1_raw[0][:], in_=w1_rows[:, :, : H // 2])
-        for q in range(4):
-            nc.sync.dma_start(
-                out=scale_table[32 * q : 32 * q + 4, :].bitcast(I32),
-                in_=x_scales[0, 4 * q : 4 * q + 4, :].bitcast(I32),
-            )
+        nc.sync.dma_start(out=scale_table[0:P:8, :].bitcast(I32), in_=x_scales[0].bitcast(I32))
         nc.sync.dma_start(out=w1_raw[1][:], in_=w1_rows[:, :, H // 2 :])
         nc.sync.dma_start(
             out=word_table[:].bitcast(I32),
             in_=x_words[0].rearrange("p n t -> p (n t)").bitcast(I32),
         )
-        for s, w in enumerate((w2, w3)):
-            nc.sync.dma_start(out=w23_raw[s][:], in_=w.rearrange("(p t) n -> p t n", t=PACK))
 
         identity = keep.tile([P, P], F32, name="identity", align_bytes=64)
         make_identity(nc, identity[:])
@@ -61,17 +58,22 @@ def tile_picked_statpool_gelu_p_kernel(tc, x_words, x_scales, w1, w2, w3, offs, 
         def list_slice(g):
             return offsets[:, g * GATHER // 16 : (g + 1) * GATHER // 16]
 
-        x_planes = [keep.tile([P, GATHER], U8, name=f"x_planes{g}", align_bytes=64) for g in range(S // GATHER)]
-        for g in range(S // GATHER):
-            nc.vector.tensor_copy(out=x_planes[g][:], in_=scale_table[:].indirect(list_slice(g)))
+        picked_scales = keep.tile([P, S], U8, name="picked_scales", align_bytes=64)
+        nc.vector.tensor_copy(out=picked_scales[:], in_=scale_table[:].indirect(offsets[:]))
+        for r in range(4):
+            nc.sync.dma_start(out=x_plane[r:P:32, :].bitcast(I32), in_=picked_scales[8 * r : P : 32, :].bitcast(I32))
 
         w1_bf = keep.tile([P, H * PACK], BF16, name="w1_bf", tag="w1_then_x", align_bytes=64)
-        w1_dealt = w1_bf[:].rearrange("p (t m j) -> p m j t", t=PACK, j=PACK)
-        for u in range(2):
-            nc.scalar.copy(
-                out=w1_dealt[:, u * P // 2 : (u + 1) * P // 2, :, :],
-                in_=w1_raw[u][:].rearrange("p j (m t) -> p m j t", t=PACK),
-            )
+        w1_dealt = w1_bf[:].rearrange("p (t m j) -> p t m j", t=PACK, j=PACK)
+        w1_from = [raw[:].rearrange("p j (m t) -> p t m j", t=PACK) for raw in w1_raw]
+        nc.scalar.copy(out=w1_dealt[:, :, 0:64, :], in_=w1_from[0])
+        nc.scalar.copy(out=w1_dealt[:, :, 64:96, :], in_=w1_from[1][:, :, 0:32, :])
+        nc.vector.tensor_copy(out=w1_dealt[:, :, 96:128, :], in_=w1_from[1][:, :, 32:64, :])
+        w23_raw = [
+            keep.tile([P, PACK, N], F32, name=f"w{2 + s}_raw", tag=f"raw{s}", align_bytes=64) for s in range(2)
+        ]
+        for s, w in enumerate((w2, w3)):
+            nc.sync.dma_start(out=w23_raw[s][:], in_=w.rearrange("(p t) n -> p t n", t=PACK))
         w1_codes = keep.tile([P, H], U32, name="w1_codes", align_bytes=64)
         w1_plane = keep.tile([P, H], U8, name="w1_plane", align_bytes=64)
         nc.vector.quantize_mx(out=w1_codes[:].bitcast(FP8X4), scales=w1_plane[:], in_=w1_bf[:])
@@ -84,39 +86,41 @@ def tile_picked_statpool_gelu_p_kernel(tc, x_words, x_scales, w1, w2, w3, offs, 
 
         w23_bf = keep.tile([P, 2, N * PACK], BF16, name="w23_bf", align_bytes=64)
         for s in range(2):
-            nc.gpsimd.tensor_scalar(
+            nc.scalar.copy(
                 out=w23_bf[:, s, :].rearrange("p (n t) -> p n t", t=PACK),
-                in0=w23_raw[s][:].rearrange("p t n -> p n t"),
-                scalar1=1.0,
-                scalar2=0.0,
-                op0=ALU.mult,
-                op1=ALU.add,
+                in_=w23_raw[s][:].rearrange("p t n -> p n t"),
             )
         w23_codes = keep.tile([P, 2 * N], U32, name="w23_codes", align_bytes=64)
         w23_plane = keep.tile([P, 2 * N], U8, name="w23_plane", align_bytes=64)
 
-        def wide(name):
-            return keep.tile([P, H], F32, name=name, align_bytes=64)
-
-        h = {}
-        val = {}
         banks = {}
 
-        def hidden(d, vt):
+        def product(d, vt):
             entry = d * V + vt * P
-            g, col = divmod(entry, GATHER)
             pre = psum.tile([P, H], F32, name=f"pre{d}_{vt}", tag="pre", bufs=3)
             nc.tensor.matmul_mx(
                 out=pre[:],
                 lhsT=x_codes[:, entry : entry + P].bitcast(FP8X4),
-                lhsT_scale=x_planes[g][:, col : col + P],
+                lhsT_scale=x_plane[:, entry : entry + P],
                 rhs=w1_codes[:].bitcast(FP8X4),
                 rhs_scale=w1_plane[:],
                 start=True,
                 stop=True,
             )
-            h[d, vt] = wide(f"h{d}_{vt}")
-            nc.scalar.activation(out=h[d, vt][:], in_=pre[:], func=ACT.Gelu_apprx_tanh)
+            banks[d, vt] = pre
+
+        h = [
+            keep.tile([P, D, H], F32, name=f"h{vt}", tag="raw1" if vt == 0 else f"h{vt}", align_bytes=64)
+            for vt in range(TILES)
+        ]
+        sums = [keep.tile([P, 2, H], F32, name=f"pair_sums{vt}", align_bytes=64) for vt in range(TILES)]
+        diffs = [keep.tile([P, 2, H], F32, name=f"pair_diffs{vt}", tag=f"pair_diffs{vt}", align_bytes=64) for vt in range(TILES)]
+        squares = [keep.tile([P, 2, H], F32, name=f"pair_squares{vt}", align_bytes=64) for vt in range(TILES)]
+        cross = [keep.tile([P, H], F32, name=f"cross{vt}", align_bytes=64) for vt in range(TILES)]
+        cross_sq = [keep.tile([P, H], F32, name=f"cross_sq{vt}", align_bytes=64) for vt in range(TILES)]
+
+        def hidden(d, vt):
+            nc.scalar.activation(out=h[vt][:, d, :], in_=banks[d, vt][:], func=ACT.Gelu_apprx_tanh)
 
         def turn_and_add(bank, values, first, last):
             for t in range(PACK):
@@ -129,49 +133,55 @@ def tile_picked_statpool_gelu_p_kernel(tc, x_words, x_scales, w1, w2, w3, offs, 
                     stop=last and t == PACK - 1,
                 )
 
-        def combine(name, vt, x, y, op):
-            val[name, vt] = wide(f"{name}{vt}")
-            nc.vector.tensor_tensor(out=val[name, vt][:], in0=x[:], in1=y[:], op=op)
+        def pairs(into, op, vt, first=0, count=2):
+            even = h[vt][:, 2 * first : 2 * (first + count) : 2, :]
+            odd = h[vt][:, 2 * first + 1 : 2 * (first + count) : 2, :]
+            nc.vector.tensor_tensor(out=into[vt][:, first : first + count, :], in0=even, in1=odd, op=op)
 
-        def first_pair(vt):
-            combine("b", vt, h[0, vt], h[1, vt], ALU.subtract)
-            combine("a", vt, h[0, vt], h[1, vt], ALU.add)
-
-        def add_square(name, vt, first, last):
-            if first:
-                banks["q", vt] = psum.tile([P, PACK, P], F32, name=f"squares{vt}", tag="squares", bufs=3)
-            turn_and_add(banks["q", vt], val[name, vt], first, last)
-
-        def scalar_square(name, vt):
-            val[2 * name, vt] = wide(f"{2 * name}{vt}")
-            nc.scalar.activation(out=val[2 * name, vt][:], in_=val[name, vt][:], func=ACT.Square)
-
-        def second_pair(vt):
-            combine("c", vt, h[2, vt], h[3, vt], ALU.add)
-            combine("e", vt, h[2, vt], h[3, vt], ALU.subtract)
+        def add_terms(vt, terms):
             banks["s", vt] = psum.tile([P, PACK, P], F32, name=f"sums{vt}", tag="sums", bufs=2)
-            turn_and_add(banks["s", vt], val["c", vt], True, False)
-            turn_and_add(banks["s", vt], val["a", vt], False, True)
-            combine("f", vt, val["a", vt], val["c", vt], ALU.subtract)
+            for n, term in enumerate(terms):
+                turn_and_add(banks["s", vt], term, n == 0, n == len(terms) - 1)
+
+        def add_sums(vt):
+            add_terms(vt, [sums[vt][:, 1, :], sums[vt][:, 0, :]])
+
+        def cross_difference(vt):
+            nc.vector.tensor_tensor(out=cross[vt][:], in0=sums[vt][:, 0, :], in1=sums[vt][:, 1, :], op=ALU.subtract)
+
+        def add_pair_squares(vt):
+            banks["q", vt] = psum.tile([P, PACK, P], F32, name=f"squares{vt}", tag="squares", bufs=3)
+            turn_and_add(banks["q", vt], squares[vt][:, 0, :], True, False)
+            turn_and_add(banks["q", vt], squares[vt][:, 1, :], False, False)
+
+        def scalar_squares(vt):
+            nc.scalar.activation(out=squares[vt][:], in_=diffs[vt][:], func=ACT.Square)
+            add_pair_squares(vt)
+
+        def vector_squares(vt):
+            nc.vector.tensor_tensor(out=squares[vt][:], in0=diffs[vt][:], in1=diffs[vt][:], op=ALU.mult)
+            add_pair_squares(vt)
 
         def half_square(vt):
-            val["ff", vt] = wide(f"ff{vt}")
             nc.vector.scalar_tensor_tensor(
-                out=val["ff", vt][:], in0=val["f", vt][:], scalar=0.5, in1=val["f", vt][:], op0=ALU.mult, op1=ALU.mult
+                out=cross_sq[vt][:], in0=cross[vt][:], scalar=0.5, in1=cross[vt][:], op0=ALU.mult, op1=ALU.mult
             )
+
+        def add_cross_square(vt):
+            turn_and_add(banks["q", vt], cross_sq[vt][:], False, True)
 
         mean_bf = keep.tile([P, TILES * H], BF16, name="mean_bf", align_bytes=64)
-        dev_bf = keep.tile([P, TILES * H], BF16, name="dev_bf", tag="w1_then_x", align_bytes=64)
+        dev_bf = keep.tile([P, TILES * H], BF16, name="dev_bf", tag="pair_diffs2", align_bytes=64)
         stat_bf = (mean_bf, dev_bf)
-        stat_codes = [keep.tile([P, 2 * P], U32, name=f"stat_codes{vt}", align_bytes=64) for vt in range(TILES)]
-        stat_plane = [keep.tile([P, 2 * P], U8, name=f"stat_plane{vt}", align_bytes=64) for vt in range(TILES)]
+        codes = {}
 
-        def quantize_stat(s, vt):
+        def quantize_stat(s, first, count):
+            words = keep.tile([P, count * P], U32, name=f"stat_codes{s}_{first}", align_bytes=64)
+            plane = keep.tile([P, count * P], U8, name=f"stat_plane{s}_{first}", align_bytes=64)
             nc.vector.quantize_mx(
-                out=stat_codes[vt][:, s * P : (s + 1) * P].bitcast(FP8X4),
-                scales=stat_plane[vt][:, s * P : (s + 1) * P],
-                in_=stat_bf[s][:, vt * H : (vt + 1) * H],
+                out=words[:].bitcast(FP8X4), scales=plane[:], in_=stat_bf[s][:, first * H : (first + count) * H]
             )
+            codes[s, first] = (words, plane)
 
         def mean(vt):
             nc.scalar.activation(
@@ -199,68 +209,65 @@ def tile_picked_statpool_gelu_p_kernel(tc, x_words, x_scales, w1, w2, w3, offs, 
                 bias=SQRT_FLOOR,
             )
 
-        def project(vt):
-            acc = psum.tile([P, H], F32, name=f"acc{vt}", tag="pre", bufs=3)
+        def project(first, count, copy):
+            width = count * P
+            acc = psum.tile([P, H], F32, name=f"acc{first}", tag="pre", bufs=3)
             for s in range(2):
+                words, plane = codes[s, first]
                 nc.tensor.matmul_mx(
-                    out=acc[:, :P],
+                    out=acc[:, :width],
                     lhsT=w23_codes[:, s * N : (s + 1) * N].bitcast(FP8X4),
                     lhsT_scale=w23_plane[:, s * N : (s + 1) * N],
-                    rhs=stat_codes[vt][:, s * P : (s + 1) * P].bitcast(FP8X4),
-                    rhs_scale=stat_plane[vt][:, s * P : (s + 1) * P],
+                    rhs=words[:].bitcast(FP8X4),
+                    rhs_scale=plane[:],
                     start=s == 0,
                     stop=s == 1,
                 )
-            result = keep.tile([P, P], F32, name=f"result{vt}")
-            nc.vector.tensor_copy(out=result[:], in_=acc[:, :P])
-            nc.sync.dma_start(out=out[:, vt * P : (vt + 1) * P], in_=result[:])
+            result = keep.tile([P, width], F32, name=f"result{first}")
+            copy(out=result[:], in_=acc[:, :width])
+            nc.sync.dma_start(out=out[:, first * P : first * P + width], in_=result[:])
 
-        for vt in range(2):
-            hidden(0, vt)
-            hidden(1, vt)
-            first_pair(vt)
-        for vt in range(2):
-            hidden(2, vt)
-            hidden(3, vt)
-        second_pair(0)
-        combine("ee", 0, val["e", 0], val["e", 0], ALU.mult)
-        half_square(0)
-        for vt in range(2):
-            scalar_square("b", vt)
-            add_square("bb", vt, True, False)
-        add_square("ee", 0, False, False)
-        add_square("ff", 0, False, True)
-        hidden(0, 2)
-        hidden(1, 2)
-        second_pair(1)
-        first_pair(2)
-        half_square(1)
-        add_square("ff", 1, False, False)
-        mean(0)
-        hidden(2, 2)
-        hidden(3, 2)
-        deviation(0)
-        scalar_square("e", 1)
-        add_square("ee", 1, False, True)
-        second_pair(2)
-        scalar_square("b", 2)
-        add_square("bb", 2, True, False)
-        mean(1)
+        for vt in range(TILES):
+            for d in range(D):
+                product(d, vt)
         nc.vector.quantize_mx(
             out=w23_codes[:].bitcast(FP8X4), scales=w23_plane[:], in_=w23_bf[:].rearrange("p s c -> p (s c)")
         )
+        for pair in range(2):
+            hidden(2 * pair, 0)
+            hidden(2 * pair + 1, 0)
+            pairs(sums, ALU.add, 0, pair, 1)
+            pairs(diffs, ALU.subtract, 0, pair, 1)
+        add_sums(0)
+        cross_difference(0)
+        vector_squares(0)
+        half_square(0)
+        add_cross_square(0)
+        for vt in (1, 2):
+            for d in range(D):
+                hidden(d, vt)
+        add_terms(2, [h[2][:, d, :] for d in range(D)])
+        pairs(diffs, ALU.subtract, 1)
+        pairs(sums, ALU.add, 1)
+        mean(0)
+        scalar_squares(1)
+        add_sums(1)
+        mean(2)
+        pairs(diffs, ALU.subtract, 2)
+        scalar_squares(2)
+        cross_difference(1)
+        pairs(sums, ALU.add, 2)
+        half_square(1)
+        add_cross_square(1)
+        cross_difference(2)
+        quantize_stat(0, 2, 1)
         half_square(2)
-        scalar_square("e", 2)
-        add_square("ff", 2, False, False)
-        add_square("ee", 2, False, True)
-        deviation(1)
-        deviation(2)
-        for vt in range(2):
-            quantize_stat(0, vt)
-        mean_on_vector(2)
-        for vt in range(2):
-            quantize_stat(1, vt)
-            project(vt)
-        quantize_stat(0, 2)
-        quantize_stat(1, 2)
-        project(2)
+        add_cross_square(2)
+        mean_on_vector(1)
+        for vt in range(TILES):
+            deviation(vt)
+        for s in range(2):
+            quantize_stat(s, 0, 2)
+        quantize_stat(1, 2, 1)
+        project(0, 2, nc.scalar.copy)
+        project(2, 1, nc.vector.tensor_copy)

@@ -19,8 +19,14 @@ ALU = mybir.AluOpType
 
 P = 128
 PACK = 4
+QUADRANT = 32
+SCALE_ROWS = 4
+ROW_STEP = P // (K // 32)
 GATHER = 512
 TILES = V // P
+MEAN, DEV = 0, 1
+SCALAR_SLOTS = 3
+PRODUCT_BANKS, SUM_BANKS, SQUARE_BANKS = 3, 2, TILES
 SQRT_FLOOR = 2.0**-116
 
 
@@ -32,19 +38,18 @@ def tile_picked_statpool_gelu_p_kernel(tc, x_words, x_scales, w1, w2, w3, offs, 
 
         offsets = keep.tile([P, S // 16], U16, name="offsets")
         word_table = keep.tile([P, T], U32, name="word_table", align_bytes=64)
-        scale_table = keep.tile([P, T], U8, name="scale_table", align_bytes=64)
-        w1_raw = [
-            keep.tile([P, PACK, H // 2], F32, name=f"w1_raw{u}", tag=f"raw{u}", align_bytes=64) for u in range(2)
-        ]
+        scale_table = keep.tile([P, T], U8, name="scale_table", tag="staging", align_bytes=64)
+        w1_raw = keep.tile([P, PACK, H], F32, name="w1_raw", align_bytes=64)
         x_plane = keep.tile([P, S], U8, name="x_plane", align_bytes=64)
 
         nc.vector.memset(scale_table[:].bitcast(I32), 0)
         nc.gpsimd.memset(x_plane[:].bitcast(I32), 0)
+
         nc.sync.dma_start(offsets[:], offs)
         w1_rows = w1.rearrange("(p j) c -> p j c", j=PACK)
-        nc.sync.dma_start(out=w1_raw[0][:], in_=w1_rows[:, :, : H // 2])
-        nc.sync.dma_start(out=scale_table[0:P:8, :].bitcast(I32), in_=x_scales[0].bitcast(I32))
-        nc.sync.dma_start(out=w1_raw[1][:], in_=w1_rows[:, :, H // 2 :])
+        nc.sync.dma_start(out=w1_raw[:, : PACK // 2, :], in_=w1_rows[:, : PACK // 2, :])
+        nc.sync.dma_start(out=scale_table[0:P:ROW_STEP, :].bitcast(I32), in_=x_scales[0].bitcast(I32))
+        nc.sync.dma_start(out=w1_raw[:, PACK // 2 :, :], in_=w1_rows[:, PACK // 2 :, :])
         nc.sync.dma_start(
             out=word_table[:].bitcast(I32),
             in_=x_words[0].rearrange("p n t -> p (n t)").bitcast(I32),
@@ -52,54 +57,69 @@ def tile_picked_statpool_gelu_p_kernel(tc, x_words, x_scales, w1, w2, w3, offs, 
 
         identity = keep.tile([P, P], F32, name="identity", align_bytes=64)
         make_identity(nc, identity[:])
-        warm = keep.tile([P, 1], F32, name="warm")
-        nc.scalar.activation(out=warm[:], in_=identity[:, 0:1], func=ACT.Gelu_apprx_tanh)
 
-        def list_slice(g):
-            return offsets[:, g * GATHER // 16 : (g + 1) * GATHER // 16]
+        zero_bias = keep.tile([P, 1], F32, name="zero_bias")
+        zero = keep.tile([P, 1], F32, name="zero")
+        nc.gpsimd.memset(zero[:], 0.0)
+        nc.scalar.activation(out=zero_bias[:], in_=zero[:], func=ACT.Gelu_apprx_tanh)
 
         picked_scales = keep.tile([P, S], U8, name="picked_scales", align_bytes=64)
         nc.vector.tensor_copy(out=picked_scales[:], in_=scale_table[:].indirect(offsets[:]))
-        for r in range(4):
-            nc.sync.dma_start(out=x_plane[r:P:32, :].bitcast(I32), in_=picked_scales[8 * r : P : 32, :].bitcast(I32))
+        for r in range(SCALE_ROWS):
+            nc.sync.dma_start(
+                out=x_plane[r:P:QUADRANT, :].bitcast(I32),
+                in_=picked_scales[ROW_STEP * r : P : QUADRANT, :].bitcast(I32),
+            )
+
+        w23_raw = keep.tile([P, 2 * PACK * N], F32, name="w23_raw", tag="staging", align_bytes=64)
+        w23_parts = [w23_raw[:, s * PACK * N : (s + 1) * PACK * N] for s in (MEAN, DEV)]
+        for part, weight in zip(w23_parts, (w2, w3)):
+            nc.sync.dma_start(out=part, in_=weight.rearrange("(p t) n -> p (t n)", t=PACK))
 
         w1_bf = keep.tile([P, H * PACK], BF16, name="w1_bf", tag="w1_then_x", align_bytes=64)
         w1_dealt = w1_bf[:].rearrange("p (t m j) -> p t m j", t=PACK, j=PACK)
-        w1_from = [raw[:].rearrange("p j (m t) -> p t m j", t=PACK) for raw in w1_raw]
-        nc.scalar.copy(out=w1_dealt[:, :, 0:64, :], in_=w1_from[0])
-        nc.scalar.copy(out=w1_dealt[:, :, 64:96, :], in_=w1_from[1][:, :, 0:32, :])
-        nc.vector.tensor_copy(out=w1_dealt[:, :, 96:128, :], in_=w1_from[1][:, :, 32:64, :])
-        w23_raw = [
-            keep.tile([P, PACK, N], F32, name=f"w{2 + s}_raw", tag=f"raw{s}", align_bytes=64) for s in range(2)
-        ]
-        for s, w in enumerate((w2, w3)):
-            nc.sync.dma_start(out=w23_raw[s][:], in_=w.rearrange("(p t) n -> p t n", t=PACK))
+        w1_from = w1_raw[:].rearrange("p j (m t) -> p t m j", t=PACK)
+        nc.scalar.copy(out=w1_dealt[:, :SCALAR_SLOTS, :, :], in_=w1_from[:, :SCALAR_SLOTS, :, :])
+        nc.vector.tensor_copy(out=w1_dealt[:, SCALAR_SLOTS, :, :], in_=w1_from[:, SCALAR_SLOTS, :, :])
         w1_codes = keep.tile([P, H], U32, name="w1_codes", align_bytes=64)
         w1_plane = keep.tile([P, H], U8, name="w1_plane", align_bytes=64)
         nc.vector.quantize_mx(out=w1_codes[:].bitcast(FP8X4), scales=w1_plane[:], in_=w1_bf[:])
 
         x_codes = keep.tile([P, S], U32, name="x_codes", tag="w1_then_x", align_bytes=64)
-        for g in range(S // GATHER):
-            nc.vector.tensor_copy(
-                out=x_codes[:, g * GATHER : (g + 1) * GATHER], in_=word_table[:].indirect(list_slice(g))
-            )
+        for start in range(0, S, GATHER):
+            entries = offsets[:, start // 16 : (start + GATHER) // 16]
+            nc.vector.tensor_copy(out=x_codes[:, start : start + GATHER], in_=word_table[:].indirect(entries))
 
         w23_bf = keep.tile([P, 2, N * PACK], BF16, name="w23_bf", align_bytes=64)
-        for s in range(2):
+        for s in (MEAN, DEV):
             nc.scalar.copy(
                 out=w23_bf[:, s, :].rearrange("p (n t) -> p n t", t=PACK),
-                in_=w23_raw[s][:].rearrange("p t n -> p n t"),
+                in_=w23_parts[s].rearrange("p (t n) -> p n t", t=PACK),
             )
         w23_codes = keep.tile([P, 2 * N], U32, name="w23_codes", align_bytes=64)
         w23_plane = keep.tile([P, 2 * N], U8, name="w23_plane", align_bytes=64)
 
-        banks = {}
+        def float_tiles(name, shape, tags):
+            return [
+                keep.tile([P, *shape], F32, name=f"{name}{vt}", tag=tags.get(vt, f"{name}{vt}"), align_bytes=64)
+                for vt in range(TILES)
+            ]
 
-        def product(d, vt):
+        h = float_tiles("h", [D, H], {0: "staging"})
+        pair_sums = float_tiles("pair_sums", [2, H], {})
+        pair_diffs = float_tiles("pair_diffs", [2, H], {TILES - 1: "diffs_then_dev"})
+        pair_squares = float_tiles("pair_squares", [2, H], {})
+        cross = float_tiles("cross", [H], {})
+        cross_square = float_tiles("cross_square", [H], {})
+        mean_bf = keep.tile([P, TILES * H], BF16, name="mean_bf", align_bytes=64)
+        dev_bf = keep.tile([P, TILES * H], BF16, name="dev_bf", tag="diffs_then_dev", align_bytes=64)
+        product_bank, sum_bank, square_bank, stat_mx = {}, {}, {}, {}
+
+        def first_product(d, vt):
             entry = d * V + vt * P
-            pre = psum.tile([P, H], F32, name=f"pre{d}_{vt}", tag="pre", bufs=3)
+            product_bank[d, vt] = psum.tile([P, H], F32, name=f"pre{d}_{vt}", tag="product", bufs=PRODUCT_BANKS)
             nc.tensor.matmul_mx(
-                out=pre[:],
+                out=product_bank[d, vt][:],
                 lhsT=x_codes[:, entry : entry + P].bitcast(FP8X4),
                 lhsT_scale=x_plane[:, entry : entry + P],
                 rhs=w1_codes[:].bitcast(FP8X4),
@@ -107,121 +127,106 @@ def tile_picked_statpool_gelu_p_kernel(tc, x_words, x_scales, w1, w2, w3, offs, 
                 start=True,
                 stop=True,
             )
-            banks[d, vt] = pre
 
-        h = [
-            keep.tile([P, D, H], F32, name=f"h{vt}", tag="raw1" if vt == 0 else f"h{vt}", align_bytes=64)
-            for vt in range(TILES)
-        ]
-        sums = [keep.tile([P, 2, H], F32, name=f"pair_sums{vt}", align_bytes=64) for vt in range(TILES)]
-        diffs = [keep.tile([P, 2, H], F32, name=f"pair_diffs{vt}", tag=f"pair_diffs{vt}", align_bytes=64) for vt in range(TILES)]
-        squares = [keep.tile([P, 2, H], F32, name=f"pair_squares{vt}", align_bytes=64) for vt in range(TILES)]
-        cross = [keep.tile([P, H], F32, name=f"cross{vt}", align_bytes=64) for vt in range(TILES)]
-        cross_sq = [keep.tile([P, H], F32, name=f"cross_sq{vt}", align_bytes=64) for vt in range(TILES)]
+        def gelu(d, vt):
+            nc.scalar.activation(
+                out=h[vt][:, d, :], in_=product_bank[d, vt][:], func=ACT.Gelu_apprx_tanh, bias=zero_bias[:]
+            )
 
-        def hidden(d, vt):
-            nc.scalar.activation(out=h[vt][:, d, :], in_=banks[d, vt][:], func=ACT.Gelu_apprx_tanh)
-
-        def turn_and_add(bank, values, first, last):
-            for t in range(PACK):
-                nc.tensor.matmul(
-                    out=bank[:, t, :],
-                    lhsT=values[:, t * P : (t + 1) * P],
-                    rhs=identity[:],
-                    is_transpose=True,
-                    start=first and t == 0,
-                    stop=last and t == PACK - 1,
-                )
-
-        def pairs(into, op, vt, first=0, count=2):
+        def combine_pairs(into, op, vt, first=0, count=2):
             even = h[vt][:, 2 * first : 2 * (first + count) : 2, :]
             odd = h[vt][:, 2 * first + 1 : 2 * (first + count) : 2, :]
             nc.vector.tensor_tensor(out=into[vt][:, first : first + count, :], in0=even, in1=odd, op=op)
 
-        def add_terms(vt, terms):
-            banks["s", vt] = psum.tile([P, PACK, P], F32, name=f"sums{vt}", tag="sums", bufs=2)
-            for n, term in enumerate(terms):
-                turn_and_add(banks["s", vt], term, n == 0, n == len(terms) - 1)
-
-        def add_sums(vt):
-            add_terms(vt, [sums[vt][:, 1, :], sums[vt][:, 0, :]])
-
         def cross_difference(vt):
-            nc.vector.tensor_tensor(out=cross[vt][:], in0=sums[vt][:, 0, :], in1=sums[vt][:, 1, :], op=ALU.subtract)
+            nc.vector.tensor_tensor(
+                out=cross[vt][:], in0=pair_sums[vt][:, 0, :], in1=pair_sums[vt][:, 1, :], op=ALU.subtract
+            )
+
+        def square_cross(vt):
+            nc.vector.scalar_tensor_tensor(
+                out=cross_square[vt][:], in0=cross[vt][:], scalar=0.5, in1=cross[vt][:], op0=ALU.mult, op1=ALU.mult
+            )
+
+        def turn_and_add(bank, terms, opens, closes):
+            for n, term in enumerate(terms):
+                for t in range(PACK):
+                    nc.tensor.matmul(
+                        out=bank[:, t, :],
+                        lhsT=term[:, t * P : (t + 1) * P],
+                        rhs=identity[:],
+                        is_transpose=True,
+                        start=opens and n == 0 and t == 0,
+                        stop=closes and n == len(terms) - 1 and t == PACK - 1,
+                    )
+
+        def add_up_h(vt, terms):
+            sum_bank[vt] = psum.tile([P, PACK, P], F32, name=f"sums{vt}", tag="sums", bufs=SUM_BANKS)
+            turn_and_add(sum_bank[vt], terms, True, True)
+
+        def add_up_pair_sums(vt):
+            add_up_h(vt, [pair_sums[vt][:, 1, :], pair_sums[vt][:, 0, :]])
 
         def add_pair_squares(vt):
-            banks["q", vt] = psum.tile([P, PACK, P], F32, name=f"squares{vt}", tag="squares", bufs=3)
-            turn_and_add(banks["q", vt], squares[vt][:, 0, :], True, False)
-            turn_and_add(banks["q", vt], squares[vt][:, 1, :], False, False)
-
-        def scalar_squares(vt):
-            nc.scalar.activation(out=squares[vt][:], in_=diffs[vt][:], func=ACT.Square)
-            add_pair_squares(vt)
-
-        def vector_squares(vt):
-            nc.vector.tensor_tensor(out=squares[vt][:], in0=diffs[vt][:], in1=diffs[vt][:], op=ALU.mult)
-            add_pair_squares(vt)
-
-        def half_square(vt):
-            nc.vector.scalar_tensor_tensor(
-                out=cross_sq[vt][:], in0=cross[vt][:], scalar=0.5, in1=cross[vt][:], op0=ALU.mult, op1=ALU.mult
-            )
+            square_bank[vt] = psum.tile([P, PACK, P], F32, name=f"squares{vt}", tag="squares", bufs=SQUARE_BANKS)
+            turn_and_add(square_bank[vt], [pair_squares[vt][:, 0, :], pair_squares[vt][:, 1, :]], True, False)
 
         def add_cross_square(vt):
-            turn_and_add(banks["q", vt], cross_sq[vt][:], False, True)
+            turn_and_add(square_bank[vt], [cross_square[vt][:]], False, True)
 
-        mean_bf = keep.tile([P, TILES * H], BF16, name="mean_bf", align_bytes=64)
-        dev_bf = keep.tile([P, TILES * H], BF16, name="dev_bf", tag="pair_diffs2", align_bytes=64)
-        stat_bf = (mean_bf, dev_bf)
-        codes = {}
+        def square_pairs_on_scalar(vt):
+            nc.scalar.activation(out=pair_squares[vt][:], in_=pair_diffs[vt][:], func=ACT.Square)
+            add_pair_squares(vt)
 
-        def quantize_stat(s, first, count):
-            words = keep.tile([P, count * P], U32, name=f"stat_codes{s}_{first}", align_bytes=64)
-            plane = keep.tile([P, count * P], U8, name=f"stat_plane{s}_{first}", align_bytes=64)
-            nc.vector.quantize_mx(
-                out=words[:].bitcast(FP8X4), scales=plane[:], in_=stat_bf[s][:, first * H : (first + count) * H]
-            )
-            codes[s, first] = (words, plane)
+        def square_pairs_on_vector(vt):
+            nc.vector.tensor_tensor(out=pair_squares[vt][:], in0=pair_diffs[vt][:], in1=pair_diffs[vt][:], op=ALU.mult)
+            add_pair_squares(vt)
 
-        def mean(vt):
+        def side_by_side(stat, vt):
+            return stat[:, vt * H : (vt + 1) * H].rearrange("p (v t) -> p v t", t=PACK)
+
+        def by_segment(bank):
+            return bank[:].rearrange("p t v -> p v t")
+
+        def mean_on_scalar(vt):
             nc.scalar.activation(
-                out=mean_bf[:, vt * H : (vt + 1) * H].rearrange("p (v t) -> p v t", t=PACK),
-                in_=banks["s", vt][:].rearrange("p t v -> p v t"),
-                func=ACT.Copy,
-                scale=1.0 / D,
+                out=side_by_side(mean_bf, vt), in_=by_segment(sum_bank[vt]), func=ACT.Copy, scale=1.0 / D
             )
 
         def mean_on_vector(vt):
             nc.vector.tensor_scalar(
-                out=mean_bf[:, vt * H : (vt + 1) * H].rearrange("p (v t) -> p v t", t=PACK),
-                in0=banks["s", vt][:].rearrange("p t v -> p v t"),
-                scalar1=1.0 / D,
-                scalar2=None,
-                op0=ALU.mult,
+                out=side_by_side(mean_bf, vt), in0=by_segment(sum_bank[vt]), scalar1=1.0 / D, scalar2=None, op0=ALU.mult
             )
 
         def deviation(vt):
             nc.scalar.activation(
-                out=dev_bf[:, vt * H : (vt + 1) * H].rearrange("p (v t) -> p v t", t=PACK),
-                in_=banks["q", vt][:].rearrange("p t v -> p v t"),
+                out=side_by_side(dev_bf, vt),
+                in_=by_segment(square_bank[vt]),
                 func=ACT.Sqrt,
                 scale=1.0 / (2 * D),
                 bias=SQRT_FLOOR,
             )
 
-        def project(first, count, copy):
+        def quantize_stat(s, first, count):
+            words = keep.tile([P, count * P], U32, name=f"stat_codes{s}_{first}", align_bytes=64)
+            plane = keep.tile([P, count * P], U8, name=f"stat_plane{s}_{first}", align_bytes=64)
+            values = (mean_bf, dev_bf)[s][:, first * H : (first + count) * H]
+            nc.vector.quantize_mx(out=words[:].bitcast(FP8X4), scales=plane[:], in_=values)
+            stat_mx[s, first] = (words, plane)
+
+        def second_product(first, count, copy):
             width = count * P
-            acc = psum.tile([P, H], F32, name=f"acc{first}", tag="pre", bufs=3)
-            for s in range(2):
-                words, plane = codes[s, first]
+            acc = psum.tile([P, H], F32, name=f"acc{first}", tag="product", bufs=PRODUCT_BANKS)
+            for s in (MEAN, DEV):
+                words, plane = stat_mx[s, first]
                 nc.tensor.matmul_mx(
                     out=acc[:, :width],
                     lhsT=w23_codes[:, s * N : (s + 1) * N].bitcast(FP8X4),
                     lhsT_scale=w23_plane[:, s * N : (s + 1) * N],
                     rhs=words[:].bitcast(FP8X4),
                     rhs_scale=plane[:],
-                    start=s == 0,
-                    stop=s == 1,
+                    start=s == MEAN,
+                    stop=s == DEV,
                 )
             result = keep.tile([P, width], F32, name=f"result{first}")
             copy(out=result[:], in_=acc[:, :width])
@@ -229,45 +234,49 @@ def tile_picked_statpool_gelu_p_kernel(tc, x_words, x_scales, w1, w2, w3, offs, 
 
         for vt in range(TILES):
             for d in range(D):
-                product(d, vt)
+                first_product(d, vt)
         nc.vector.quantize_mx(
             out=w23_codes[:].bitcast(FP8X4), scales=w23_plane[:], in_=w23_bf[:].rearrange("p s c -> p (s c)")
         )
-        for pair in range(2):
-            hidden(2 * pair, 0)
-            hidden(2 * pair + 1, 0)
-            pairs(sums, ALU.add, 0, pair, 1)
-            pairs(diffs, ALU.subtract, 0, pair, 1)
-        add_sums(0)
-        cross_difference(0)
-        vector_squares(0)
-        half_square(0)
-        add_cross_square(0)
-        for vt in (1, 2):
+
+        first, middle, last = range(TILES)
+        for pair in range(D // 2):
+            gelu(2 * pair, first)
+            gelu(2 * pair + 1, first)
+            combine_pairs(pair_sums, ALU.add, first, pair, 1)
+            combine_pairs(pair_diffs, ALU.subtract, first, pair, 1)
+        add_up_pair_sums(first)
+        cross_difference(first)
+        square_pairs_on_vector(first)
+        square_cross(first)
+        add_cross_square(first)
+
+        for vt in (middle, last):
             for d in range(D):
-                hidden(d, vt)
-        add_terms(2, [h[2][:, d, :] for d in range(D)])
-        pairs(diffs, ALU.subtract, 1)
-        pairs(sums, ALU.add, 1)
-        mean(0)
-        scalar_squares(1)
-        add_sums(1)
-        mean(2)
-        pairs(diffs, ALU.subtract, 2)
-        scalar_squares(2)
-        cross_difference(1)
-        pairs(sums, ALU.add, 2)
-        half_square(1)
-        add_cross_square(1)
-        cross_difference(2)
-        quantize_stat(0, 2, 1)
-        half_square(2)
-        add_cross_square(2)
-        mean_on_vector(1)
+                gelu(d, vt)
+        add_up_h(last, [h[last][:, d, :] for d in range(D)])
+        combine_pairs(pair_diffs, ALU.subtract, middle)
+        combine_pairs(pair_sums, ALU.add, middle)
+        mean_on_scalar(first)
+        square_pairs_on_scalar(middle)
+        add_up_pair_sums(middle)
+        mean_on_scalar(last)
+        combine_pairs(pair_diffs, ALU.subtract, last)
+        square_pairs_on_scalar(last)
+        cross_difference(middle)
+        combine_pairs(pair_sums, ALU.add, last)
+        square_cross(middle)
+        add_cross_square(middle)
+        cross_difference(last)
+        quantize_stat(MEAN, last, 1)
+        square_cross(last)
+        add_cross_square(last)
+
+        mean_on_vector(middle)
         for vt in range(TILES):
             deviation(vt)
-        for s in range(2):
-            quantize_stat(s, 0, 2)
-        quantize_stat(1, 2, 1)
-        project(0, 2, nc.scalar.copy)
-        project(2, 1, nc.vector.tensor_copy)
+        for s in (MEAN, DEV):
+            quantize_stat(s, first, 2)
+        quantize_stat(DEV, last, 1)
+        second_product(first, 2, nc.scalar.copy)
+        second_product(last, 1, nc.vector.tensor_copy)

from contextlib import ExitStack

import concourse.mybir as mybir
from concourse.masks import make_identity

K, T, S, V, H, N = 512, 4096, 1536, 384, 512, 128
D = S // V
FLOPS = 2 * K * H * S + 2 * 2 * H * N * V

F32 = mybir.dt.float32
BF16 = mybir.dt.bfloat16
I32 = mybir.dt.int32
U32 = mybir.dt.uint32
U16 = mybir.dt.uint16
U8 = mybir.dt.uint8
FP8X4 = mybir.dt.float8_e4m3fn_x4
ACT = mybir.ActivationFunctionType
ALU = mybir.AluOpType

P = 128
PACK = 4
QUADRANT = 32
SCALE_ROWS = 4
ROW_STEP = P // (K // 32)
GATHER = 512
TILES = V // P
MEAN, DEV = 0, 1
SCALAR_SLOTS = 3
PRODUCT_BANKS, SUM_BANKS, SQUARE_BANKS = 3, 2, TILES
SQRT_FLOOR = 2.0**-116


def tile_picked_statpool_gelu_p_kernel(tc, x_words, x_scales, w1, w2, w3, offs, out):
    nc = tc.nc
    with ExitStack() as ctx:
        keep = ctx.enter_context(tc.tile_pool(name="keep", bufs=1))
        psum = ctx.enter_context(tc.psum_pool(name="psum", bufs=1))

        offsets = keep.tile([P, S // 16], U16, name="offsets")
        word_table = keep.tile([P, T], U32, name="word_table", align_bytes=64)
        scale_table = keep.tile([P, T], U8, name="scale_table", tag="staging", align_bytes=64)
        w1_raw = keep.tile([P, PACK, H], F32, name="w1_raw", align_bytes=64)
        x_plane = keep.tile([P, S], U8, name="x_plane", align_bytes=64)

        nc.vector.memset(scale_table[:].bitcast(I32), 0)
        nc.gpsimd.memset(x_plane[:].bitcast(I32), 0)

        nc.sync.dma_start(offsets[:], offs)
        w1_rows = w1.rearrange("(p j) c -> p j c", j=PACK)
        nc.sync.dma_start(out=w1_raw[:, : PACK // 2, :], in_=w1_rows[:, : PACK // 2, :])
        nc.sync.dma_start(out=scale_table[0:P:ROW_STEP, :].bitcast(I32), in_=x_scales[0].bitcast(I32))
        nc.sync.dma_start(out=w1_raw[:, PACK // 2 :, :], in_=w1_rows[:, PACK // 2 :, :])
        nc.sync.dma_start(
            out=word_table[:].bitcast(I32),
            in_=x_words[0].rearrange("p n t -> p (n t)").bitcast(I32),
        )

        identity = keep.tile([P, P], F32, name="identity", align_bytes=64)
        make_identity(nc, identity[:])

        zero_bias = keep.tile([P, 1], F32, name="zero_bias")
        zero = keep.tile([P, 1], F32, name="zero")
        nc.gpsimd.memset(zero[:], 0.0)
        nc.scalar.activation(out=zero_bias[:], in_=zero[:], func=ACT.Gelu_apprx_tanh)

        picked_scales = keep.tile([P, S], U8, name="picked_scales", align_bytes=64)
        nc.vector.tensor_copy(out=picked_scales[:], in_=scale_table[:].indirect(offsets[:]))
        for r in range(SCALE_ROWS):
            nc.sync.dma_start(
                out=x_plane[r:P:QUADRANT, :].bitcast(I32),
                in_=picked_scales[ROW_STEP * r : P : QUADRANT, :].bitcast(I32),
            )

        w23_raw = keep.tile([P, 2 * PACK * N], F32, name="w23_raw", tag="staging", align_bytes=64)
        w23_parts = [w23_raw[:, s * PACK * N : (s + 1) * PACK * N] for s in (MEAN, DEV)]
        for part, weight in zip(w23_parts, (w2, w3)):
            nc.sync.dma_start(out=part, in_=weight.rearrange("(p t) n -> p (t n)", t=PACK))

        w1_bf = keep.tile([P, H * PACK], BF16, name="w1_bf", tag="w1_then_x", align_bytes=64)
        w1_dealt = w1_bf[:].rearrange("p (t m j) -> p t m j", t=PACK, j=PACK)
        w1_from = w1_raw[:].rearrange("p j (m t) -> p t m j", t=PACK)
        nc.scalar.copy(out=w1_dealt[:, :SCALAR_SLOTS, :, :], in_=w1_from[:, :SCALAR_SLOTS, :, :])
        nc.vector.tensor_copy(out=w1_dealt[:, SCALAR_SLOTS, :, :], in_=w1_from[:, SCALAR_SLOTS, :, :])
        w1_codes = keep.tile([P, H], U32, name="w1_codes", align_bytes=64)
        w1_plane = keep.tile([P, H], U8, name="w1_plane", align_bytes=64)
        nc.vector.quantize_mx(out=w1_codes[:].bitcast(FP8X4), scales=w1_plane[:], in_=w1_bf[:])

        x_codes = keep.tile([P, S], U32, name="x_codes", tag="w1_then_x", align_bytes=64)
        for start in range(0, S, GATHER):
            entries = offsets[:, start // 16 : (start + GATHER) // 16]
            nc.vector.tensor_copy(out=x_codes[:, start : start + GATHER], in_=word_table[:].indirect(entries))

        w23_bf = keep.tile([P, 2, N * PACK], BF16, name="w23_bf", align_bytes=64)
        for s in (MEAN, DEV):
            nc.scalar.copy(
                out=w23_bf[:, s, :].rearrange("p (n t) -> p n t", t=PACK),
                in_=w23_parts[s].rearrange("p (t n) -> p n t", t=PACK),
            )
        w23_codes = keep.tile([P, 2 * N], U32, name="w23_codes", align_bytes=64)
        w23_plane = keep.tile([P, 2 * N], U8, name="w23_plane", align_bytes=64)

        def float_tiles(name, shape, tags):
            return [
                keep.tile([P, *shape], F32, name=f"{name}{vt}", tag=tags.get(vt, f"{name}{vt}"), align_bytes=64)
                for vt in range(TILES)
            ]

        h = float_tiles("h", [D, H], {0: "staging"})
        pair_sums = float_tiles("pair_sums", [2, H], {})
        pair_diffs = float_tiles("pair_diffs", [2, H], {TILES - 1: "diffs_then_dev"})
        pair_squares = float_tiles("pair_squares", [2, H], {})
        cross = float_tiles("cross", [H], {})
        cross_square = float_tiles("cross_square", [H], {})
        mean_bf = keep.tile([P, TILES * H], BF16, name="mean_bf", align_bytes=64)
        dev_bf = keep.tile([P, TILES * H], BF16, name="dev_bf", tag="diffs_then_dev", align_bytes=64)
        product_bank, sum_bank, square_bank, stat_mx = {}, {}, {}, {}

        def first_product(d, vt):
            entry = d * V + vt * P
            product_bank[d, vt] = psum.tile([P, H], F32, name=f"pre{d}_{vt}", tag="product", bufs=PRODUCT_BANKS)
            nc.tensor.matmul_mx(
                out=product_bank[d, vt][:],
                lhsT=x_codes[:, entry : entry + P].bitcast(FP8X4),
                lhsT_scale=x_plane[:, entry : entry + P],
                rhs=w1_codes[:].bitcast(FP8X4),
                rhs_scale=w1_plane[:],
                start=True,
                stop=True,
            )

        def gelu(d, vt):
            nc.scalar.activation(
                out=h[vt][:, d, :], in_=product_bank[d, vt][:], func=ACT.Gelu_apprx_tanh, bias=zero_bias[:]
            )

        def combine_pairs(into, op, vt, first=0, count=2):
            even = h[vt][:, 2 * first : 2 * (first + count) : 2, :]
            odd = h[vt][:, 2 * first + 1 : 2 * (first + count) : 2, :]
            nc.vector.tensor_tensor(out=into[vt][:, first : first + count, :], in0=even, in1=odd, op=op)

        def cross_difference(vt):
            nc.vector.tensor_tensor(
                out=cross[vt][:], in0=pair_sums[vt][:, 0, :], in1=pair_sums[vt][:, 1, :], op=ALU.subtract
            )

        def square_cross(vt):
            nc.vector.scalar_tensor_tensor(
                out=cross_square[vt][:], in0=cross[vt][:], scalar=0.5, in1=cross[vt][:], op0=ALU.mult, op1=ALU.mult
            )

        def turn_and_add(bank, terms, opens, closes):
            for n, term in enumerate(terms):
                for t in range(PACK):
                    nc.tensor.matmul(
                        out=bank[:, t, :],
                        lhsT=term[:, t * P : (t + 1) * P],
                        rhs=identity[:],
                        is_transpose=True,
                        start=opens and n == 0 and t == 0,
                        stop=closes and n == len(terms) - 1 and t == PACK - 1,
                    )

        def add_up_h(vt, terms):
            sum_bank[vt] = psum.tile([P, PACK, P], F32, name=f"sums{vt}", tag="sums", bufs=SUM_BANKS)
            turn_and_add(sum_bank[vt], terms, True, True)

        def add_up_pair_sums(vt):
            add_up_h(vt, [pair_sums[vt][:, 1, :], pair_sums[vt][:, 0, :]])

        def add_pair_squares(vt):
            square_bank[vt] = psum.tile([P, PACK, P], F32, name=f"squares{vt}", tag="squares", bufs=SQUARE_BANKS)
            turn_and_add(square_bank[vt], [pair_squares[vt][:, 0, :], pair_squares[vt][:, 1, :]], True, False)

        def add_cross_square(vt):
            turn_and_add(square_bank[vt], [cross_square[vt][:]], False, True)

        def square_pairs_on_scalar(vt):
            nc.scalar.activation(out=pair_squares[vt][:], in_=pair_diffs[vt][:], func=ACT.Square)
            add_pair_squares(vt)

        def square_pairs_on_vector(vt):
            nc.vector.tensor_tensor(out=pair_squares[vt][:], in0=pair_diffs[vt][:], in1=pair_diffs[vt][:], op=ALU.mult)
            add_pair_squares(vt)

        def side_by_side(stat, vt):
            return stat[:, vt * H : (vt + 1) * H].rearrange("p (v t) -> p v t", t=PACK)

        def by_segment(bank):
            return bank[:].rearrange("p t v -> p v t")

        def mean_on_scalar(vt):
            nc.scalar.activation(
                out=side_by_side(mean_bf, vt), in_=by_segment(sum_bank[vt]), func=ACT.Copy, scale=1.0 / D
            )

        def mean_on_vector(vt):
            nc.vector.tensor_scalar(
                out=side_by_side(mean_bf, vt), in0=by_segment(sum_bank[vt]), scalar1=1.0 / D, scalar2=None, op0=ALU.mult
            )

        def deviation(vt):
            nc.scalar.activation(
                out=side_by_side(dev_bf, vt),
                in_=by_segment(square_bank[vt]),
                func=ACT.Sqrt,
                scale=1.0 / (2 * D),
                bias=SQRT_FLOOR,
            )

        def quantize_stat(s, first, count):
            words = keep.tile([P, count * P], U32, name=f"stat_codes{s}_{first}", align_bytes=64)
            plane = keep.tile([P, count * P], U8, name=f"stat_plane{s}_{first}", align_bytes=64)
            values = (mean_bf, dev_bf)[s][:, first * H : (first + count) * H]
            nc.vector.quantize_mx(out=words[:].bitcast(FP8X4), scales=plane[:], in_=values)
            stat_mx[s, first] = (words, plane)

        def second_product(first, count, copy):
            width = count * P
            acc = psum.tile([P, H], F32, name=f"acc{first}", tag="product", bufs=PRODUCT_BANKS)
            for s in (MEAN, DEV):
                words, plane = stat_mx[s, first]
                nc.tensor.matmul_mx(
                    out=acc[:, :width],
                    lhsT=w23_codes[:, s * N : (s + 1) * N].bitcast(FP8X4),
                    lhsT_scale=w23_plane[:, s * N : (s + 1) * N],
                    rhs=words[:].bitcast(FP8X4),
                    rhs_scale=plane[:],
                    start=s == MEAN,
                    stop=s == DEV,
                )
            result = keep.tile([P, width], F32, name=f"result{first}")
            copy(out=result[:], in_=acc[:, :width])
            nc.sync.dma_start(out=out[:, first * P : first * P + width], in_=result[:])

        for vt in range(TILES):
            for d in range(D):
                first_product(d, vt)
        nc.vector.quantize_mx(
            out=w23_codes[:].bitcast(FP8X4), scales=w23_plane[:], in_=w23_bf[:].rearrange("p s c -> p (s c)")
        )

        first, middle, last = range(TILES)
        for pair in range(D // 2):
            gelu(2 * pair, first)
            gelu(2 * pair + 1, first)
            combine_pairs(pair_sums, ALU.add, first, pair, 1)
            combine_pairs(pair_diffs, ALU.subtract, first, pair, 1)
        add_up_pair_sums(first)
        cross_difference(first)
        square_pairs_on_vector(first)
        square_cross(first)
        add_cross_square(first)

        for vt in (middle, last):
            for d in range(D):
                gelu(d, vt)
        add_up_h(last, [h[last][:, d, :] for d in range(D)])
        combine_pairs(pair_diffs, ALU.subtract, middle)
        combine_pairs(pair_sums, ALU.add, middle)
        mean_on_scalar(first)
        square_pairs_on_scalar(middle)
        add_up_pair_sums(middle)
        mean_on_scalar(last)
        combine_pairs(pair_diffs, ALU.subtract, last)
        square_pairs_on_scalar(last)
        cross_difference(middle)
        combine_pairs(pair_sums, ALU.add, last)
        square_cross(middle)
        add_cross_square(middle)
        cross_difference(last)
        quantize_stat(MEAN, last, 1)
        square_cross(last)
        add_cross_square(last)

        mean_on_vector(middle)
        for vt in range(TILES):
            deviation(vt)
        for s in (MEAN, DEV):
            quantize_stat(s, first, 2)
        quantize_stat(DEV, last, 1)
        second_product(first, 2, nc.scalar.copy)
        second_product(last, 1, nc.vector.tensor_copy)
